import numpy as np
import ml_dtypes


def mxq(x, axis, fmt="e4m3"):
    dtype, down = {"e4m3": (ml_dtypes.float8_e4m3fn, 7), "e5m2": (ml_dtypes.float8_e5m2, 14)}[fmt]
    v = np.moveaxis(np.asarray(x, np.float32).astype(ml_dtypes.bfloat16).astype(np.float64), axis, -1)
    blocks = v.reshape(v.shape[:-1] + (-1, 32))
    amax = np.abs(blocks).max(-1, keepdims=True)
    byte = np.maximum(np.where(amax > 0, np.frexp(amax)[1] - 1 + 127, 0) - down, 1)
    scale = np.exp2(byte - 127.0)
    codes = (blocks / scale).astype(np.float32).astype(dtype).astype(np.float64)
    return np.moveaxis((codes * scale).reshape(v.shape), -1, axis)


WIDE = False


def mx_kscale(k):
    if not WIDE:
        return np.ones(k)
    levels = np.array([10, -10, 5, -5, 0])
    if k % 512:
        return np.exp2(np.random.permutation(np.resize(levels, k // 32))).repeat(32)
    a = np.empty((k // 512, 16))
    for p in range(k // 512):
        a[p, :8] = np.random.permutation(np.resize(levels, 8))
        for g in range(8):
            far = levels[np.abs(levels - a[p, g]) >= 10]
            a[p, g + 8] = far[np.random.randint(len(far))]
    return np.exp2(a.ravel()).repeat(32)


def f64(x):
    return np.asarray(x).astype(np.float64)


def striped(idx):
    return np.tile(idx.reshape(-1, 16).T, (8, 1)).astype(np.uint16)


def unstriped(offs):
    return offs[:16].T.reshape(-1).astype(np.int64)


E2M1 = np.array([0.0, 0.5, 1.0, 1.5, 2.0, 3.0, 4.0, 6.0, -0.0, -0.5, -1.0, -1.5, -2.0, -3.0, -4.0, -6.0])


def pack_weight(w, fmt):
    k, n = w.shape
    w = f64(np.asarray(w, np.float32).astype(ml_dtypes.bfloat16)).reshape(k // 32, 32, n)
    amax = np.abs(w).max(1)
    if fmt == "e4m3":
        byte = np.frexp(amax)[1] - 1 + 127 - 7
    else:
        mant, ex = np.frexp(amax / 6.0)
        byte = np.where(mant > 0.5, ex, ex - 1) + 127
    byte = np.clip(np.where(amax > 0, byte, 1), 1, 254)
    scaled = (w * np.exp2(127.0 - byte)[:, None, :]).reshape(k, n).astype(np.float32)
    by_word = np.ascontiguousarray(scaled.reshape(k // 512, 128, 4, n).transpose(0, 1, 3, 2))
    if fmt == "e4m3":
        words = by_word.astype(ml_dtypes.float8_e4m3fn).view(np.uint8)
    else:
        c = by_word.astype(ml_dtypes.float4_e2m1fn).view(np.uint8) & 0xF
        words = (c[..., 0::2] | (c[..., 1::2] << 4)).reshape(k // 512, 128, 2 * n)
    return np.ascontiguousarray(words), np.ascontiguousarray(byte.astype(np.uint8).reshape(k // 512, 16, n))


def unpack_weight(words, scales, fmt):
    g, _, n = scales.shape
    words = np.ascontiguousarray(words).reshape(g, 128, n, -1)
    if fmt == "e4m3":
        vals = words.view(ml_dtypes.float8_e4m3fn).astype(np.float64)
    else:
        nib = np.empty((g, 128, n, 4), np.uint8)
        nib[..., 0::2] = words & 0xF
        nib[..., 1::2] = words >> 4
        vals = E2M1[nib]
    vals = vals * np.repeat(np.exp2(scales.astype(np.float64) - 127.0), 8, axis=1)[..., None]
    return vals.transpose(0, 1, 3, 2).reshape(g * 512, n)


def gelu(v):
    return 0.5 * v * (1.0 + np.tanh(np.sqrt(2.0 / np.pi) * (v + 0.044715 * v**3)))


def bf(x):
    return np.asarray(x, np.float32).astype(ml_dtypes.bfloat16)


def planes(Y):
    n, m = Y.shape
    b = f64(bf(Y)).reshape(n // 32, 32, m)
    amax = np.abs(b).max(1)
    byte = np.clip(np.where(amax > 0, np.frexp(amax)[1] - 1 + 127 - 7, 1), 1, 254)
    codes = (b * np.exp2(127.0 - byte)[:, None, :]).reshape(n, m).astype(np.float32).astype(ml_dtypes.float8_e4m3fn).view(np.uint8)
    words = codes.reshape(n // 512, 128, 4, m).transpose(0, 1, 3, 2)
    return np.ascontiguousarray(words), np.ascontiguousarray(byte.astype(np.uint8).reshape(n // 512, 16, m))


K, H, N, T, S, T2, P = 1024, 1024, 384, 2048, 1024, 2048, 512

def setup_inputs():
    n = np.random.standard_normal
    s = mx_kscale(K)[:, None]
    u = mx_kscale(H)[:, None]
    d = {}
    d["tab_words"], d["tab_scales"] = pack_weight(n((K, T)) * s, "e4m3")
    d["offs"] = striped(np.random.permutation(T)[:S])
    d["w1"] = (0.8 * n((K, H)) / K ** 0.5 / s * u.T).astype(np.float32)
    d["w2_words"], d["w2_scales"] = pack_weight(n((K, H)) / K ** 0.5 / s, "e2m1")
    d["alloy"] = np.random.uniform(0.4, 1.6, (H, S)).astype(np.float32)
    d["page0"] = (n((H, T2)) * u).astype(np.float32)
    d["wgs"] = np.exp(0.3 * n((128, S))).astype(np.float32)
    d["offs2"] = striped(np.random.permutation(T2)[:S])
    d["offs3"] = striped(np.random.permutation(T2)[:P])
    d["tau"] = (0.5 * n(H) * u[:, 0]).astype(np.float32)
    d["w3"] = (1.2 * n((H, N)) / H ** 0.5 / u).astype(np.float32)
    d["span"] = np.random.uniform(1.3, 2.4, N).astype(np.float32)
    return d

def reference(tab_words, tab_scales, offs, w1, w2_words, w2_scales, alloy, page0, wgs, offs2, offs3, tau, w3, span):
    v = unpack_weight(tab_words, tab_scales, "e4m3")[:, unstriped(offs)]
    a = mxq(f64(w1), 0, "e4m3").T @ v
    b = unpack_weight(w2_words, w2_scales, "e2m1").T @ v
    h = a * f64(alloy) * b + a
    page = f64(page0).copy()
    page[:, unstriped(offs2)] = np.tile(f64(wgs), (H // 128, 1)) * h
    x = np.maximum(page[:, unstriped(offs3)], f64(tau)[:, None])
    g = mxq(f64(w3), 0, "e4m3").T @ mxq(x, 0, "e4m3")
    y = np.cos(f64(span)[:, None] * np.tanh(g))
    words, scales = planes(page)
    return y, page, words, scales

@@ -1,0 +1,360 @@
+import math
+from contextlib import ExitStack
+
+import concourse.mybir as mybir
+
+K, H, N, T, S, T2, PK = 1024, 1024, 384, 2048, 1024, 2048, 512
+FLOPS = 2 * K * H * S * 2 + 2 * H * N * PK
+
+F32 = mybir.dt.float32
+BF16 = mybir.dt.bfloat16
+I32 = mybir.dt.int32
+U32 = mybir.dt.uint32
+U16 = mybir.dt.uint16
+U8 = mybir.dt.uint8
+FP8X4 = mybir.dt.float8_e4m3fn_x4
+FP4X4 = mybir.dt.float4_e2m1fn_x4
+ALU = mybir.AluOpType
+ACT = mybir.ActivationFunctionType
+
+P = 128
+PACK = 4
+GROUP = P * PACK
+BANK = 512
+PASSES = K // GROUP
+GROUPS = H // GROUP
+SLICES = GROUPS * PACK
+HALVES = S // BANK
+CHUNKS = T2 // BANK
+NT = N // P
+
+
+def tile_list_reed_bench_page_kernel(
+    tc, tab_words, tab_scales, offs, w1, w2_words, w2_scales, alloy, page0, wgs, offs2, offs3, tau, w3, span,
+    out_0, out_1, out_2, out_3,
+):
+    nc = tc.nc
+    with ExitStack() as ctx:
+        lists = ctx.enter_context(tc.tile_pool(name="lists", bufs=1))
+        keep = ctx.enter_context(tc.tile_pool(name="keep", bufs=1))
+        ring = ctx.enter_context(tc.tile_pool(name="ring", bufs=2))
+        psum = ctx.enter_context(tc.psum_pool(name="psum", bufs=4))
+
+        def dealt(mat, s):
+            g, t = divmod(s, PACK)
+            return mat[g * GROUP : (g + 1) * GROUP, :].rearrange("(p t) c -> t p c", t=PACK)[t]
+
+        idx = lists.tile([P, S // 16], U16, name="idx")
+        idx2 = lists.tile([P, S // 16], U16, name="idx2")
+        idx3 = lists.tile([P, PK // 16], U16, name="idx3")
+        nc.sync.dma_start(idx[:], offs)
+        nc.sync.dma_start(idx2[:], offs2)
+        nc.sync.dma_start(idx3[:], offs3)
+        tau_sb = keep.tile([P, GROUPS, PACK], F32, name="tau_sb")
+        nc.sync.dma_start(tau_sb[:], tau.rearrange("(g p t) -> p g t", g=GROUPS, t=PACK))
+        span_sb = keep.tile([P, NT], F32, name="span_sb")
+        with nc.allow_non_contiguous_dma(reason="one value of span for each partition"):
+            nc.sync.dma_start(span_sb[:], span.rearrange("(c p) -> p c", p=P))
+
+        tab_s = keep.tile([P, PASSES, T], U8, name="tab_s", align_bytes=64)
+        w2_s = keep.tile([P, PASSES, H], U8, name="w2_s", align_bytes=64)
+        nc.vector.memset(tab_s[:].rearrange("p a c -> p (a c)").bitcast(I32), 0)
+        nc.gpsimd.memset(w2_s[:].rearrange("p a c -> p (a c)").bitcast(I32), 0)
+        for q in range(4):
+            nc.sync.dma_start(
+                tab_s[32 * q : 32 * q + 4].bitcast(I32),
+                tab_scales[:, 4 * q : 4 * q + 4, :].rearrange("a r c -> r a c").bitcast(I32),
+            )
+        for q in range(4):
+            nc.sync.dma_start(
+                w2_s[32 * q : 32 * q + 4].bitcast(I32),
+                w2_scales[:, 4 * q : 4 * q + 4, :].rearrange("a r c -> r a c").bitcast(I32),
+            )
+        w2_w = [keep.tile([P, PASSES, 2 * GROUP], U8, name="w2_w%d" % g, align_bytes=64) for g in range(GROUPS)]
+
+        def load_w2(g):
+            cols = w2_words[:, :, 2 * g * GROUP : 2 * (g + 1) * GROUP]
+            nc.sync.dma_start(w2_w[g][:].bitcast(I32), cols.rearrange("a p c -> p a c").bitcast(I32))
+
+        load_w2(0)
+
+        tab_w = [keep.tile([P, T], I32, name="tab_w%d" % a, align_bytes=64) for a in range(PASSES)]
+
+        def load_tab(a):
+            nc.sync.dma_start(tab_w[a][:], tab_words[a].rearrange("p c i -> p (c i)").bitcast(I32))
+
+        w_raw = {}
+
+        def load_w1(g, a):
+            w_raw[g, a] = ring.tile([P, PACK, GROUP], F32, name="w_raw", tag="w_raw", bufs=3)
+            rows = w1[a * GROUP : (a + 1) * GROUP, g * GROUP : (g + 1) * GROUP]
+            nc.sync.dma_start(w_raw[g, a][:], rows.rearrange("(p j) c -> p j c", j=PACK))
+
+        alloy_sb, page = {}, {}
+
+        def load_alloy(s):
+            alloy_sb[s] = ring.tile([P, S], F32, name="alloy_sb", tag="alloy_sb", bufs=3)
+            nc.sync.dma_start(alloy_sb[s][:], dealt(alloy, s))
+
+        def load_page(s):
+            page[s] = ring.tile([P, T2], F32, name="page", bufs=4)
+            nc.sync.dma_start(page[s][:], dealt(page0, s))
+
+        wgs_first = keep.tile([P, S], F32, name="wgs_first")
+        wgs_rest = keep.tile([P, PACK - 1, S], F32, name="wgs_rest")
+        wgs_rows = wgs.rearrange("(p t) c -> p t c", t=PACK)
+
+        load_tab(0)
+        load_tab(1)
+        load_w1(0, 0)
+        load_w1(0, 1)
+        load_alloy(0)
+        load_alloy(1)
+        load_w2(1)
+        for q in (0, 2, 1, 3):
+            nc.sync.dma_start(wgs_first[32 * q : 32 * q + 32, :], wgs_rows[:, 0, :])
+        load_page(0)
+        load_alloy(2)
+        for q in (0, 2, 1, 3):
+            nc.sync.dma_start(wgs_rest[32 * q : 32 * q + 32], wgs_rows[:, 1:PACK, :])
+        load_page(1)
+
+        v_s = [keep.tile([P, S], U8, name="v_s%d" % a, align_bytes=64) for a in range(PASSES)]
+        v_w = [keep.tile([P, S], U32, name="v_w%d" % a, align_bytes=64) for a in range(PASSES)]
+        for a in range(PASSES):
+            nc.vector.tensor_copy(v_s[a][:], tab_s[:, a, :].indirect(idx[:]))
+        w2_sd = keep.tile([P, PASSES, SLICES, P], U8, name="w2_sd", align_bytes=64)
+        nc.vector.tensor_copy(
+            w2_sd[:].rearrange("p a (g t) m -> p (a g) t m", t=PACK),
+            w2_s[:].rearrange("p a (g m t) -> p (a g) t m", g=GROUPS, t=PACK),
+        )
+        w2_wd = [keep.tile([P, PASSES, PACK, 2 * P], U8, name="w2_wd%d" % g, align_bytes=64) for g in range(GROUPS)]
+
+        def deal_w2(g):
+            nc.vector.tensor_copy(
+                w2_wd[g][:].bitcast(U16), w2_w[g][:].bitcast(U16).rearrange("p a (m t) -> p a t m", t=PACK)
+            )
+
+        deal_w2(0)
+        for a in range(PASSES):
+            for h in range(HALVES):
+                nc.vector.tensor_copy(
+                    v_w[a][:, h * BANK : (h + 1) * BANK],
+                    tab_w[a][:].bitcast(U32).indirect(idx[:, h * BANK // 16 : (h + 1) * BANK // 16]),
+                )
+
+        w1_c, w1_s = {}, {}
+
+        w1_bf = {}
+        width = PACK * GROUP
+
+        def weave_w1(g):
+            w1_bf[g] = keep.tile([P, PASSES * width], BF16, name="w1_bf", tag="after0", align_bytes=64)
+            for a in range(PASSES):
+                nc.scalar.copy(
+                    w1_bf[g][:, a * width : (a + 1) * width].rearrange("p (t m j) -> p m j t", t=PACK, j=PACK),
+                    w_raw[g, a][:].rearrange("p j (m t) -> p m j t", t=PACK),
+                )
+
+        def quantize_w1(g):
+            codes = keep.tile([P, PASSES * GROUP], U32, name="w1_c", tag="after1" if g else "w1_c", align_bytes=64)
+            for a in range(PASSES):
+                w1_c[g, a] = codes[:, a * GROUP : (a + 1) * GROUP]
+                w1_s[g, a] = keep.tile([P, GROUP], U8, name="w1_s%d%d" % (g, a), align_bytes=64)
+                nc.vector.quantize_mx(
+                    out=w1_c[g, a].bitcast(FP8X4), scales=w1_s[g, a][:], in_=w1_bf[g][:, a * width : (a + 1) * width]
+                )
+
+        weave_w1(0)
+        quantize_w1(0)
+
+        a_ps, gate, hval, val, b_tile = {}, {}, {}, {}, {}
+
+        def parts(s):
+            return [slice(h * BANK, (h + 1) * BANK) for h in range(HALVES)] if s == 0 else [slice(0, S)]
+
+        def products(s):
+            g, t = divmod(s, PACK)
+            gate[s] = ring.tile([P, S], F32, name="gate")
+            if s > 0:
+                b_tile[s] = ring.tile([P, S], F32, name="b_sb", tag="b_sb", bufs=3)
+            for h in range(HALVES):
+                cols = slice(h * BANK, (h + 1) * BANK)
+                b_ps = psum.tile([P, BANK], F32, name="b_ps", tag="b_ps")
+                for a in range(PASSES):
+                    nc.tensor.matmul_mx(
+                        out=b_ps[:], lhsT=w2_wd[g][:, a, t, :].bitcast(FP4X4), lhsT_scale=w2_sd[:, a, s, :],
+                        rhs=v_w[a][:, cols].bitcast(FP8X4), rhs_scale=v_s[a][:, cols],
+                        start=(a == 0), stop=(a == PASSES - 1),
+                    )
+                if s == 0:
+                    nc.vector.tensor_tensor(gate[s][:, cols], b_ps[:], alloy_sb[s][:, cols], ALU.mult)
+                else:
+                    nc.scalar.copy(b_tile[s][:, cols], b_ps[:])
+            for h in range(HALVES):
+                cols = slice(h * BANK, (h + 1) * BANK)
+                a_ps[s, h] = psum.tile([P, BANK], F32, name="a_ps", tag="a_ps")
+                for a in range(PASSES):
+                    nc.tensor.matmul_mx(
+                        out=a_ps[s, h][:], lhsT=w1_c[g, a][:, t * P : (t + 1) * P].bitcast(FP8X4),
+                        lhsT_scale=w1_s[g, a][:, t * P : (t + 1) * P],
+                        rhs=v_w[a][:, cols].bitcast(FP8X4), rhs_scale=v_s[a][:, cols],
+                        start=(a == 0), stop=(a == PASSES - 1),
+                    )
+            if s > 0:
+                nc.gpsimd.tensor_tensor(gate[s][:], b_tile[s][:], alloy_sb[s][:], ALU.mult)
+
+        def combine(s):
+            hval[s] = ring.tile([P, S], F32, name="hval", tag="hval")
+            for h in range(HALVES):
+                cols = slice(h * BANK, (h + 1) * BANK)
+                nc.vector.scalar_tensor_tensor(
+                    hval[s][:, cols], gate[s][:, cols], 1.0, a_ps[s, h][:], ALU.add, ALU.mult
+                )
+
+        def weigh(s):
+            t = s % PACK
+            w_rows = wgs_first[:] if t == 0 else wgs_rest[:, t - 1, :]
+            if s + 1 < SLICES:
+                val[s] = b_tile[s + 1]
+            else:
+                val[s] = ring.tile([P, S], F32, name="val", tag="b_sb", bufs=3)
+            for cols in parts(s):
+                nc.gpsimd.tensor_tensor(val[s][:, cols], hval[s][:, cols], w_rows[:, cols], ALU.mult)
+
+        page_bf, x_bf = {}, {}
+
+        def place(s):
+            g, t = divmod(s, PACK)
+            for cols in parts(s):
+                nc.vector.tensor_copy(
+                    page[s][:].indirect(idx2[:, cols.start // 16 : cols.stop // 16]), val[s][:, cols]
+                )
+            if s <= PACK:
+                picked = keep.tile([P, PK], F32, name="picked", tag="after%d" % s, align_bytes=64)
+            else:
+                picked = ring.tile([P, PK], F32, name="picked")
+            nc.vector.tensor_copy(picked[:], page[s][:].indirect(idx3[:]))
+            if t == 0:
+                page_bf[g] = ring.tile([P, PACK, T2], BF16, name="page_bf", bufs=1)
+                x_bf[g] = ring.tile([P, PACK, PK], BF16, name="x_bf", bufs=1)
+            nc.vector.tensor_scalar(x_bf[g][:, t, :], picked[:], tau_sb[:, g, t : t + 1], None, ALU.max)
+            nc.sync.dma_start(dealt(out_1, s), page[s][:])
+            if s == SLICES - 1:
+                for c in range(CHUNKS):
+                    cols = slice(c * BANK, (c + 1) * BANK)
+                    nc.scalar.copy(page_bf[g][:, t, cols], page[s][:, cols])
+            else:
+                nc.scalar.copy(page_bf[g][:, t, :], page[s][:])
+
+        def weave(engine_copy, dst, src):
+            engine_copy(
+                dst.rearrange("p (c i t) -> p c t i", i=PACK, t=PACK),
+                src.rearrange("p t (c i) -> p c t i", i=PACK),
+            )
+
+        x_c, x_s = {}, {}
+
+        x_woven = {}
+
+        def weave_x(g):
+            x_woven[g] = keep.tile([P, PACK * PK], BF16, name="x_woven", align_bytes=64)
+            weave(nc.vector.tensor_copy if g == GROUPS - 1 else nc.scalar.copy, x_woven[g][:], x_bf[g][:])
+
+        def quantize_x(g):
+            woven = x_woven[g]
+            x_c[g] = keep.tile([P, PK], U32, name="x_c", tag="x_c" if g else "after4", align_bytes=64)
+            x_s[g] = keep.tile([P, PK], U8, name="x_s%d" % g, align_bytes=64)
+            nc.vector.quantize_mx(out=x_c[g][:].bitcast(FP8X4), scales=x_s[g][:], in_=woven[:])
+
+        def planes(g):
+            y_s = ring.tile([P, T2], U8, name="y_s", align_bytes=64)
+            words_out = out_2[g].rearrange("p m t -> p (m t)").bitcast(I32)
+            for c in range(CHUNKS):
+                cols = slice(c * BANK, (c + 1) * BANK)
+                woven = ring.tile([P, PACK * BANK], BF16, name="woven", tag="woven", bufs=3, align_bytes=64)
+                on_vector = g == GROUPS - 1 and c > 0
+                weave(nc.vector.tensor_copy if on_vector else nc.scalar.copy, woven[:], page_bf[g][:, :, cols])
+                y_c = ring.tile([P, BANK], U32, name="y_c", bufs=3, align_bytes=64)
+                nc.vector.quantize_mx(out=y_c[:].bitcast(FP8X4), scales=y_s[:, cols], in_=woven[:])
+                nc.sync.dma_start(words_out[:, cols], y_c[:].bitcast(I32))
+            for q in range(4):
+                nc.sync.dma_start(
+                    out_3[g, 4 * q : 4 * q + 4, :].bitcast(I32), y_s[32 * q : 32 * q + 4, :].bitcast(I32)
+                )
+
+        w3_s = keep.tile([P, GROUPS * N], U8, name="w3_s", align_bytes=64)
+        w3_t = {}
+        turns = keep.tile([P, NT], F32, name="turns")
+
+        def weave_w3():
+            w3_bf = keep.tile([P, GROUPS * N * PACK], BF16, name="w3_bf", tag="after2", align_bytes=64)
+            w3_t["bf"] = w3_bf
+            for g in range(GROUPS):
+                raw = ring.tile([P, PACK, N], F32, name="w_raw", tag="w_raw", bufs=3)
+                nc.sync.dma_start(raw[:], w3[g * GROUP : (g + 1) * GROUP, :].rearrange("(p j) c -> p j c", j=PACK))
+                weave(nc.scalar.copy, w3_bf[:, g * N * PACK : (g + 1) * N * PACK], raw[:])
+
+        def quantize_w3():
+            w3_bf = w3_t["bf"]
+            w3_c = keep.tile([P, GROUPS * N], U32, name="w3_c", tag="after3", align_bytes=64)
+            w3_t["c"] = w3_c
+            for lo, hi in ((0, BANK), (BANK, GROUPS * N)):
+                nc.vector.quantize_mx(
+                    out=w3_c[:, lo:hi].bitcast(FP8X4), scales=w3_s[:, lo:hi], in_=w3_bf[:, PACK * lo : PACK * hi]
+                )
+            nc.vector.tensor_scalar(turns[:], span_sb[:], 1.0 / (2.0 * math.pi), None, ALU.mult)
+
+        products(0)
+        deal_w2(1)
+        combine(0)
+        for s in range(SLICES):
+            if s == 0:
+                load_w1(1, 0)
+                load_w1(1, 1)
+            if s + 2 < SLICES:
+                load_page(s + 2)
+            if s + 1 < SLICES:
+                products(s + 1)
+            weigh(s)
+            if s + 1 < SLICES:
+                combine(s + 1)
+            if s + 3 < SLICES:
+                load_alloy(s + 3)
+            place(s)
+            if s == 0:
+                weave_w1(1)
+            if s == 1:
+                quantize_w1(1)
+            if s == 2:
+                weave_w3()
+            if s == PACK - 1:
+                quantize_w3()
+                weave_x(0)
+                planes(0)
+            if s == PACK:
+                quantize_x(0)
+
+        weave_x(1)
+        quantize_x(1)
+        g_ps = [psum.tile([P, BANK], F32, name="g_ps", tag="b_ps") for c in range(NT)]
+        for g in range(GROUPS):
+            for c in range(NT):
+                cols = slice(g * N + c * P, g * N + (c + 1) * P)
+                nc.tensor.matmul_mx(
+                    out=g_ps[c][:], lhsT=w3_t["c"][:, cols].bitcast(FP8X4), lhsT_scale=w3_s[:, cols],
+                    rhs=x_c[g][:].bitcast(FP8X4), rhs_scale=x_s[g][:],
+                    start=(g == 0), stop=(g == GROUPS - 1),
+                )
+        for c in range(NT):
+            th = ring.tile([P, PK], F32, name="th", tag="alloy_sb", bufs=3)
+            nc.scalar.activation(th[:], g_ps[c][:], ACT.Tanh)
+            whole = ring.tile([P, PK], I32, name="whole", tag="b_sb", bufs=3)
+            nc.vector.tensor_scalar(whole[:], th[:], turns[:, c : c + 1], None, ALU.mult)
+            rest = ring.tile([P, PK], F32, name="rest", tag="hval")
+            nc.vector.scalar_tensor_tensor(rest[:], th[:], turns[:, c : c + 1], whole[:], ALU.mult, ALU.subtract)
+            nc.scalar.activation(th[:], rest[:], ACT.Abs)
+            y = ring.tile([P, PK], F32, name="y", tag="w_raw", bufs=3)
+            nc.scalar.activation(y[:], th[:], ACT.Sin, bias=math.pi / 2.0, scale=-2.0 * math.pi)
+            nc.sync.dma_start(out_0[c * P : (c + 1) * P, :], y[:])
+        planes(1)

@@ -38,6 +38,7 @@ def tile_list_reed_bench_page_kernel(
         lists = ctx.enter_context(tc.tile_pool(name="lists", bufs=1))
         keep = ctx.enter_context(tc.tile_pool(name="keep", bufs=1))
         ring = ctx.enter_context(tc.tile_pool(name="ring", bufs=2))
+        late = ctx.enter_context(tc.tile_pool(name="late", bufs=1))
         psum = ctx.enter_context(tc.psum_pool(name="psum", bufs=4))
 
         def dealt(mat, s):
@@ -47,36 +48,19 @@ def tile_list_reed_bench_page_kernel(
         idx = lists.tile([P, S // 16], U16, name="idx")
         idx2 = lists.tile([P, S // 16], U16, name="idx2")
         idx3 = lists.tile([P, PK // 16], U16, name="idx3")
-        nc.sync.dma_start(idx[:], offs)
-        nc.sync.dma_start(idx2[:], offs2)
-        nc.sync.dma_start(idx3[:], offs3)
-        tau_sb = keep.tile([P, GROUPS, PACK], F32, name="tau_sb")
-        nc.sync.dma_start(tau_sb[:], tau.rearrange("(g p t) -> p g t", g=GROUPS, t=PACK))
-        span_sb = keep.tile([P, NT], F32, name="span_sb")
-        with nc.allow_non_contiguous_dma(reason="one value of span for each partition"):
-            nc.sync.dma_start(span_sb[:], span.rearrange("(c p) -> p c", p=P))
-
         tab_s = keep.tile([P, PASSES, T], U8, name="tab_s", align_bytes=64)
-        w2_s = keep.tile([P, PASSES, H], U8, name="w2_s", align_bytes=64)
-        nc.vector.memset(tab_s[:].rearrange("p a c -> p (a c)").bitcast(I32), 0)
+        w2_s = late.tile([P, PASSES, H], U8, name="w2_s", align_bytes=64, offset=3072)
+        nc.gpsimd.memset(tab_s[:].rearrange("p a c -> p (a c)").bitcast(I32), 0)
         nc.gpsimd.memset(w2_s[:].rearrange("p a c -> p (a c)").bitcast(I32), 0)
-        for q in range(4):
-            nc.sync.dma_start(
-                tab_s[32 * q : 32 * q + 4].bitcast(I32),
-                tab_scales[:, 4 * q : 4 * q + 4, :].rearrange("a r c -> r a c").bitcast(I32),
-            )
-        for q in range(4):
-            nc.sync.dma_start(
-                w2_s[32 * q : 32 * q + 4].bitcast(I32),
-                w2_scales[:, 4 * q : 4 * q + 4, :].rearrange("a r c -> r a c").bitcast(I32),
-            )
+        warm = keep.tile([P, 1], F32, name="warm")
+        nc.vector.memset(warm[:], 0.0)
+        nc.scalar.activation(warm[:], warm[:], ACT.Silu)
+
         w2_w = [keep.tile([P, PASSES, 2 * GROUP], U8, name="w2_w%d" % g, align_bytes=64) for g in range(GROUPS)]
 
         def load_w2(g):
             cols = w2_words[:, :, 2 * g * GROUP : 2 * (g + 1) * GROUP]
             nc.sync.dma_start(w2_w[g][:].bitcast(I32), cols.rearrange("a p c -> p a c").bitcast(I32))
-
-        load_w2(0)
 
         tab_w = [keep.tile([P, T], I32, name="tab_w%d" % a, align_bytes=64) for a in range(PASSES)]
 
@@ -104,25 +88,53 @@ def tile_list_reed_bench_page_kernel(
         wgs_rest = keep.tile([P, PACK - 1, S], F32, name="wgs_rest")
         wgs_rows = wgs.rearrange("(p t) c -> p t c", t=PACK)
 
+        nc.sync.dma_start(idx[:], offs)
+        nc.sync.dma_start(idx2[:], offs2)
+        nc.sync.dma_start(idx3[:], offs3)
+        tau_sb = keep.tile([P, GROUPS, PACK], F32, name="tau_sb")
+        nc.sync.dma_start(tau_sb[:], tau.rearrange("(g p t) -> p g t", g=GROUPS, t=PACK))
+        span_sb = keep.tile([P, NT], F32, name="span_sb")
+        with nc.allow_non_contiguous_dma(reason="one value of span for each partition"):
+            nc.sync.dma_start(span_sb[:], span.rearrange("(c p) -> p c", p=P))
+        load_w2(0)
+        load_w2(1)
         load_tab(0)
+        for q in range(4):
+            nc.sync.dma_start(
+                tab_s[32 * q : 32 * q + 4].bitcast(I32),
+                tab_scales[:, 4 * q : 4 * q + 4, :].rearrange("a r c -> r a c").bitcast(I32),
+            )
         load_tab(1)
+        for q in range(4):
+            nc.sync.dma_start(
+                w2_s[32 * q : 32 * q + 4].bitcast(I32),
+                w2_scales[:, 4 * q : 4 * q + 4, :].rearrange("a r c -> r a c").bitcast(I32),
+            )
         load_w1(0, 0)
         load_w1(0, 1)
         load_alloy(0)
         load_alloy(1)
-        load_w2(1)
         for q in (0, 2, 1, 3):
             nc.sync.dma_start(wgs_first[32 * q : 32 * q + 32, :], wgs_rows[:, 0, :])
         load_page(0)
         load_alloy(2)
         for q in (0, 2, 1, 3):
             nc.sync.dma_start(wgs_rest[32 * q : 32 * q + 32], wgs_rows[:, 1:PACK, :])
+        load_w1(1, 0)
+        load_w1(1, 1)
         load_page(1)
 
-        v_s = [keep.tile([P, S], U8, name="v_s%d" % a, align_bytes=64) for a in range(PASSES)]
-        v_w = [keep.tile([P, S], U32, name="v_w%d" % a, align_bytes=64) for a in range(PASSES)]
-        for a in range(PASSES):
-            nc.vector.tensor_copy(v_s[a][:], tab_s[:, a, :].indirect(idx[:]))
+        v_w, v_s = {}, {}
+
+        def gather_table(h):
+            entries = idx[:, h * BANK // 16 : (h + 1) * BANK // 16]
+            for a in range(PASSES):
+                nc.vector.tensor_copy(v_w[h][:, a, :], tab_w[a][:].bitcast(U32).indirect(entries))
+                nc.vector.tensor_copy(v_s[h][:, a, :], tab_s[:, a, :].indirect(entries))
+
+        v_w[0] = keep.tile([P, PASSES, BANK], U32, name="v_w0", align_bytes=64)
+        v_s[0] = keep.tile([P, PASSES, BANK], U8, name="v_s0", align_bytes=64)
+        gather_table(0)
         w2_sd = keep.tile([P, PASSES, SLICES, P], U8, name="w2_sd", align_bytes=64)
         nc.vector.tensor_copy(
             w2_sd[:].rearrange("p a (g t) m -> p (a g) t m", t=PACK),
@@ -136,12 +148,9 @@ def tile_list_reed_bench_page_kernel(
             )
 
         deal_w2(0)
-        for a in range(PASSES):
-            for h in range(HALVES):
-                nc.vector.tensor_copy(
-                    v_w[a][:, h * BANK : (h + 1) * BANK],
-                    tab_w[a][:].bitcast(U32).indirect(idx[:, h * BANK // 16 : (h + 1) * BANK // 16]),
-                )
+        v_w[1] = late.tile([P, PASSES, BANK], U32, name="v_w1", align_bytes=64, offset=0)
+        v_s[1] = late.tile([P, PASSES, BANK], U8, name="v_s1", align_bytes=64, offset=4096)
+        gather_table(1)
 
         w1_c, w1_s = {}, {}
 
@@ -168,15 +177,16 @@ def tile_list_reed_bench_page_kernel(
         weave_w1(0)
         quantize_w1(0)
 
-        a_ps, gate, hval, val, b_tile = {}, {}, {}, {}, {}
+        a_ps, gate, hval, val, b_tile, a_sb = {}, {}, {}, {}, {}, {}
 
         def parts(s):
             return [slice(h * BANK, (h + 1) * BANK) for h in range(HALVES)] if s == 0 else [slice(0, S)]
 
-        def products(s):
+        def product_b(s):
             g, t = divmod(s, PACK)
-            gate[s] = ring.tile([P, S], F32, name="gate")
-            if s > 0:
+            if s == 0:
+                gate[s] = ring.tile([P, S], F32, name="gate")
+            else:
                 b_tile[s] = ring.tile([P, S], F32, name="b_sb", tag="b_sb", bufs=3)
             for h in range(HALVES):
                 cols = slice(h * BANK, (h + 1) * BANK)
@@ -184,13 +194,21 @@ def tile_list_reed_bench_page_kernel(
                 for a in range(PASSES):
                     nc.tensor.matmul_mx(
                         out=b_ps[:], lhsT=w2_wd[g][:, a, t, :].bitcast(FP4X4), lhsT_scale=w2_sd[:, a, s, :],
-                        rhs=v_w[a][:, cols].bitcast(FP8X4), rhs_scale=v_s[a][:, cols],
+                        rhs=v_w[h][:, a, :].bitcast(FP8X4), rhs_scale=v_s[h][:, a, :],
                         start=(a == 0), stop=(a == PASSES - 1),
                     )
                 if s == 0:
                     nc.vector.tensor_tensor(gate[s][:, cols], b_ps[:], alloy_sb[s][:, cols], ALU.mult)
                 else:
                     nc.scalar.copy(b_tile[s][:, cols], b_ps[:])
+
+        def make_gate(s):
+            gate[s] = ring.tile([P, S], F32, name="gate")
+            for cols in parts(s - 1):
+                nc.gpsimd.tensor_tensor(gate[s][:, cols], b_tile[s][:, cols], alloy_sb[s][:, cols], ALU.mult)
+
+        def product_a(s):
+            g, t = divmod(s, PACK)
             for h in range(HALVES):
                 cols = slice(h * BANK, (h + 1) * BANK)
                 a_ps[s, h] = psum.tile([P, BANK], F32, name="a_ps", tag="a_ps")
@@ -198,19 +216,24 @@ def tile_list_reed_bench_page_kernel(
                     nc.tensor.matmul_mx(
                         out=a_ps[s, h][:], lhsT=w1_c[g, a][:, t * P : (t + 1) * P].bitcast(FP8X4),
                         lhsT_scale=w1_s[g, a][:, t * P : (t + 1) * P],
-                        rhs=v_w[a][:, cols].bitcast(FP8X4), rhs_scale=v_s[a][:, cols],
+                        rhs=v_w[h][:, a, :].bitcast(FP8X4), rhs_scale=v_s[h][:, a, :],
                         start=(a == 0), stop=(a == PASSES - 1),
                     )
-            if s > 0:
-                nc.gpsimd.tensor_tensor(gate[s][:], b_tile[s][:], alloy_sb[s][:], ALU.mult)
+            if s >= 2:
+                a_sb[s] = ring.tile([P, BANK], F32, name="a_sb", bufs=1)
+                nc.scalar.copy(a_sb[s][:], a_ps[s, 1][:])
 
         def combine(s):
             hval[s] = ring.tile([P, S], F32, name="hval", tag="hval")
             for h in range(HALVES):
                 cols = slice(h * BANK, (h + 1) * BANK)
-                nc.vector.scalar_tensor_tensor(
-                    hval[s][:, cols], gate[s][:, cols], 1.0, a_ps[s, h][:], ALU.add, ALU.mult
-                )
+                if h == 0 or s < 2:
+                    nc.vector.scalar_tensor_tensor(
+                        hval[s][:, cols], gate[s][:, cols], 1.0, a_ps[s, h][:], ALU.add, ALU.mult
+                    )
+                else:
+                    nc.scalar.activation(gate[s][:, cols], gate[s][:, cols], ACT.Identity, bias=1.0)
+                    nc.gpsimd.tensor_tensor(hval[s][:, cols], gate[s][:, cols], a_sb[s][:], ALU.mult)
 
         def weigh(s):
             t = s % PACK
@@ -230,10 +253,7 @@ def tile_list_reed_bench_page_kernel(
                 nc.vector.tensor_copy(
                     page[s][:].indirect(idx2[:, cols.start // 16 : cols.stop // 16]), val[s][:, cols]
                 )
-            if s <= PACK:
-                picked = keep.tile([P, PK], F32, name="picked", tag="after%d" % s, align_bytes=64)
-            else:
-                picked = ring.tile([P, PK], F32, name="picked")
+            picked = keep.tile([P, PK], F32, name="picked", tag="after%d" % (s if s < SLICES - 1 else 2), align_bytes=64)
             nc.vector.tensor_copy(picked[:], page[s][:].indirect(idx3[:]))
             if t == 0:
                 page_bf[g] = ring.tile([P, PACK, T2], BF16, name="page_bf", bufs=1)
@@ -267,21 +287,29 @@ def tile_list_reed_bench_page_kernel(
             x_s[g] = keep.tile([P, PK], U8, name="x_s%d" % g, align_bytes=64)
             nc.vector.quantize_mx(out=x_c[g][:].bitcast(FP8X4), scales=x_s[g][:], in_=woven[:])
 
-        def planes(g):
-            y_s = ring.tile([P, T2], U8, name="y_s", align_bytes=64)
+        y_s, y_woven = {}, {}
+
+        def weave_page(g, c):
+            y_woven[g, c] = ring.tile([P, PACK * BANK], BF16, name="woven", tag="woven", bufs=4, align_bytes=64)
+            on_vector = g == GROUPS - 1 and c > 0
+            cols = slice(c * BANK, (c + 1) * BANK)
+            weave(nc.vector.tensor_copy if on_vector else nc.scalar.copy, y_woven[g, c][:], page_bf[g][:, :, cols])
+
+        def planes(g, chunks, tag):
+            if chunks[0] == 0:
+                y_s[g] = ring.tile([P, T2], U8, name="y_s", bufs=1, align_bytes=64)
             words_out = out_2[g].rearrange("p m t -> p (m t)").bitcast(I32)
-            for c in range(CHUNKS):
+            y_c = keep.tile([P, len(chunks) * BANK], U32, name="y_c", tag=tag, align_bytes=64)
+            for i, c in enumerate(chunks):
                 cols = slice(c * BANK, (c + 1) * BANK)
-                woven = ring.tile([P, PACK * BANK], BF16, name="woven", tag="woven", bufs=3, align_bytes=64)
-                on_vector = g == GROUPS - 1 and c > 0
-                weave(nc.vector.tensor_copy if on_vector else nc.scalar.copy, woven[:], page_bf[g][:, :, cols])
-                y_c = ring.tile([P, BANK], U32, name="y_c", bufs=3, align_bytes=64)
-                nc.vector.quantize_mx(out=y_c[:].bitcast(FP8X4), scales=y_s[:, cols], in_=woven[:])
-                nc.sync.dma_start(words_out[:, cols], y_c[:].bitcast(I32))
-            for q in range(4):
-                nc.sync.dma_start(
-                    out_3[g, 4 * q : 4 * q + 4, :].bitcast(I32), y_s[32 * q : 32 * q + 4, :].bitcast(I32)
-                )
+                words = y_c[:, i * BANK : (i + 1) * BANK]
+                nc.vector.quantize_mx(out=words.bitcast(FP8X4), scales=y_s[g][:, cols], in_=y_woven[g, c][:])
+                nc.sync.dma_start(words_out[:, cols], words.bitcast(I32))
+            if chunks[-1] == CHUNKS - 1:
+                for q in range(4):
+                    nc.sync.dma_start(
+                        out_3[g, 4 * q : 4 * q + 4, :].bitcast(I32), y_s[g][32 * q : 32 * q + 4, :].bitcast(I32)
+                    )
 
         w3_s = keep.tile([P, GROUPS * N], U8, name="w3_s", align_bytes=64)
         w3_t = {}
@@ -305,17 +333,20 @@ def tile_list_reed_bench_page_kernel(
                 )
             nc.vector.tensor_scalar(turns[:], span_sb[:], 1.0 / (2.0 * math.pi), None, ALU.mult)
 
-        products(0)
+        product_b(0)
+        product_b(1)
+        product_a(0)
         deal_w2(1)
+        product_b(2)
         combine(0)
         for s in range(SLICES):
-            if s == 0:
-                load_w1(1, 0)
-                load_w1(1, 1)
             if s + 2 < SLICES:
                 load_page(s + 2)
+            if s + 3 < SLICES:
+                product_b(s + 3)
             if s + 1 < SLICES:
-                products(s + 1)
+                make_gate(s + 1)
+                product_a(s + 1)
             weigh(s)
             if s + 1 < SLICES:
                 combine(s + 1)
@@ -330,10 +361,17 @@ def tile_list_reed_bench_page_kernel(
                 weave_w3()
             if s == PACK - 1:
                 quantize_w3()
-                weave_x(0)
-                planes(0)
             if s == PACK:
+                weave_x(0)
                 quantize_x(0)
+            if s == PACK + 1:
+                weave_page(0, 0)
+                weave_page(0, 1)
+                planes(0, [0, 1], "after5")
+            if s == PACK + 2:
+                weave_page(0, 2)
+                weave_page(0, 3)
+                planes(0, [2, 3], "after6")
 
         weave_x(1)
         quantize_x(1)
@@ -357,4 +395,7 @@ def tile_list_reed_bench_page_kernel(
             y = ring.tile([P, PK], F32, name="y", tag="w_raw", bufs=3)
             nc.scalar.activation(y[:], th[:], ACT.Sin, bias=math.pi / 2.0, scale=-2.0 * math.pi)
             nc.sync.dma_start(out_0[c * P : (c + 1) * P, :], y[:])
-        planes(1)
+        for c in range(CHUNKS):
+            weave_page(1, c)
+        planes(1, [0, 1], "after5")
+        planes(1, [2, 3], "after0")

@@ -27,6 +27,7 @@ SLICES = GROUPS * PACK
 HALVES = S // BANK
 CHUNKS = T2 // BANK
 NT = N // P
+TAIL_ON_SCALAR = 768
 
 
 def tile_list_reed_bench_page_kernel(
@@ -39,7 +40,7 @@ def tile_list_reed_bench_page_kernel(
         keep = ctx.enter_context(tc.tile_pool(name="keep", bufs=1))
         ring = ctx.enter_context(tc.tile_pool(name="ring", bufs=2))
         late = ctx.enter_context(tc.tile_pool(name="late", bufs=1))
-        psum = ctx.enter_context(tc.psum_pool(name="psum", bufs=4))
+        psum = ctx.enter_context(tc.psum_pool(name="psum", bufs=1))
 
         def dealt(mat, s):
             g, t = divmod(s, PACK)
@@ -48,10 +49,12 @@ def tile_list_reed_bench_page_kernel(
         idx = lists.tile([P, S // 16], U16, name="idx")
         idx2 = lists.tile([P, S // 16], U16, name="idx2")
         idx3 = lists.tile([P, PK // 16], U16, name="idx3")
-        tab_s = keep.tile([P, PASSES, T], U8, name="tab_s", align_bytes=64)
-        w2_s = late.tile([P, PASSES, H], U8, name="w2_s", align_bytes=64, offset=3072)
-        nc.gpsimd.memset(tab_s[:].rearrange("p a c -> p (a c)").bitcast(I32), 0)
+        tab_s = keep.tile([P, T], U8, name="tab_s", align_bytes=64)
+        v_s = [keep.tile([P, S], U8, name="v_s%d" % a, align_bytes=64) for a in range(PASSES)]
+        w2_s = late.tile([P, PASSES, H], U8, name="w2_s", align_bytes=64, offset=0)
+        nc.gpsimd.memset(tab_s[:].bitcast(I32), 0)
         nc.gpsimd.memset(w2_s[:].rearrange("p a c -> p (a c)").bitcast(I32), 0)
+        nc.gpsimd.memset(v_s[1][:].bitcast(I32), 0)
         warm = keep.tile([P, 1], F32, name="warm")
         nc.vector.memset(warm[:], 0.0)
         nc.scalar.activation(warm[:], warm[:], ACT.Silu)
@@ -84,9 +87,11 @@ def tile_list_reed_bench_page_kernel(
             page[s] = ring.tile([P, T2], F32, name="page", bufs=4)
             nc.sync.dma_start(page[s][:], dealt(page0, s))
 
-        wgs_first = keep.tile([P, S], F32, name="wgs_first")
-        wgs_rest = keep.tile([P, PACK - 1, S], F32, name="wgs_rest")
-        wgs_rows = wgs.rearrange("(p t) c -> p t c", t=PACK)
+        wgs_sb = [keep.tile([P, S], F32, name="wgs_sb%d" % t) for t in range(PACK)]
+
+        def load_wgs(t):
+            for q in (0, 2, 1, 3):
+                nc.sync.dma_start(wgs_sb[t][32 * q : 32 * q + 32, :], wgs.rearrange("(p t) c -> t p c", t=PACK)[t])
 
         nc.sync.dma_start(idx[:], offs)
         nc.sync.dma_start(idx2[:], offs2)
@@ -101,8 +106,8 @@ def tile_list_reed_bench_page_kernel(
         load_tab(0)
         for q in range(4):
             nc.sync.dma_start(
-                tab_s[32 * q : 32 * q + 4].bitcast(I32),
-                tab_scales[:, 4 * q : 4 * q + 4, :].rearrange("a r c -> r a c").bitcast(I32),
+                tab_s[32 * q : 32 * q + 4 * PASSES, :].bitcast(I32),
+                tab_scales[:, 4 * q : 4 * q + 4, :].bitcast(I32),
             )
         load_tab(1)
         for q in range(4):
@@ -114,26 +119,28 @@ def tile_list_reed_bench_page_kernel(
         load_w1(0, 1)
         load_alloy(0)
         load_alloy(1)
-        for q in (0, 2, 1, 3):
-            nc.sync.dma_start(wgs_first[32 * q : 32 * q + 32, :], wgs_rows[:, 0, :])
+        load_wgs(0)
         load_page(0)
         load_alloy(2)
-        for q in (0, 2, 1, 3):
-            nc.sync.dma_start(wgs_rest[32 * q : 32 * q + 32], wgs_rows[:, 1:PACK, :])
+        load_wgs(1)
         load_w1(1, 0)
         load_w1(1, 1)
         load_page(1)
+        load_wgs(2)
 
-        v_w, v_s = {}, {}
+        v_w = {}
+        nc.vector.tensor_copy(v_s[0][:], tab_s[:].indirect(idx[:]))
+        for q in range(4):
+            nc.scalar.dma_start(
+                v_s[1][32 * q : 32 * q + 4, :].bitcast(I32), v_s[0][32 * q + 4 : 32 * q + 8, :].bitcast(I32)
+            )
 
         def gather_table(h):
             entries = idx[:, h * BANK // 16 : (h + 1) * BANK // 16]
             for a in range(PASSES):
                 nc.vector.tensor_copy(v_w[h][:, a, :], tab_w[a][:].bitcast(U32).indirect(entries))
-                nc.vector.tensor_copy(v_s[h][:, a, :], tab_s[:, a, :].indirect(entries))
 
         v_w[0] = keep.tile([P, PASSES, BANK], U32, name="v_w0", align_bytes=64)
-        v_s[0] = keep.tile([P, PASSES, BANK], U8, name="v_s0", align_bytes=64)
         gather_table(0)
         w2_sd = keep.tile([P, PASSES, SLICES, P], U8, name="w2_sd", align_bytes=64)
         nc.vector.tensor_copy(
@@ -149,7 +156,6 @@ def tile_list_reed_bench_page_kernel(
 
         deal_w2(0)
         v_w[1] = late.tile([P, PASSES, BANK], U32, name="v_w1", align_bytes=64, offset=0)
-        v_s[1] = late.tile([P, PASSES, BANK], U8, name="v_s1", align_bytes=64, offset=4096)
         gather_table(1)
 
         w1_c, w1_s = {}, {}
@@ -182,25 +188,29 @@ def tile_list_reed_bench_page_kernel(
         def parts(s):
             return [slice(h * BANK, (h + 1) * BANK) for h in range(HALVES)] if s == 0 else [slice(0, S)]
 
-        def product_b(s):
+        def bank(s, h, which):
+            pair = 2 * ((s // 2 + which) % 2) + s % 2
+            return psum.tile([P, BANK], F32, name="acc", tag="bank%d" % (2 * pair + h))
+
+        def product_b(s, h):
             g, t = divmod(s, PACK)
-            if s == 0:
-                gate[s] = ring.tile([P, S], F32, name="gate")
-            else:
-                b_tile[s] = ring.tile([P, S], F32, name="b_sb", tag="b_sb", bufs=3)
-            for h in range(HALVES):
-                cols = slice(h * BANK, (h + 1) * BANK)
-                b_ps = psum.tile([P, BANK], F32, name="b_ps", tag="b_ps")
-                for a in range(PASSES):
-                    nc.tensor.matmul_mx(
-                        out=b_ps[:], lhsT=w2_wd[g][:, a, t, :].bitcast(FP4X4), lhsT_scale=w2_sd[:, a, s, :],
-                        rhs=v_w[h][:, a, :].bitcast(FP8X4), rhs_scale=v_s[h][:, a, :],
-                        start=(a == 0), stop=(a == PASSES - 1),
-                    )
+            if h == 0:
                 if s == 0:
-                    nc.vector.tensor_tensor(gate[s][:, cols], b_ps[:], alloy_sb[s][:, cols], ALU.mult)
+                    gate[s] = ring.tile([P, S], F32, name="gate")
                 else:
-                    nc.scalar.copy(b_tile[s][:, cols], b_ps[:])
+                    b_tile[s] = ring.tile([P, S], F32, name="b_sb", tag="b_sb", bufs=3)
+            cols = slice(h * BANK, (h + 1) * BANK)
+            b_ps = bank(s, h, 0)
+            for a in range(PASSES):
+                nc.tensor.matmul_mx(
+                    out=b_ps[:], lhsT=w2_wd[g][:, a, t, :].bitcast(FP4X4), lhsT_scale=w2_sd[:, a, s, :],
+                    rhs=v_w[h][:, a, :].bitcast(FP8X4), rhs_scale=v_s[a][:, cols],
+                    start=(a == 0), stop=(a == PASSES - 1),
+                )
+            if s == 0:
+                nc.vector.tensor_tensor(gate[s][:, cols], b_ps[:], alloy_sb[s][:, cols], ALU.mult)
+            else:
+                nc.scalar.copy(b_tile[s][:, cols], b_ps[:])
 
         def make_gate(s):
             gate[s] = ring.tile([P, S], F32, name="gate")
@@ -210,13 +220,12 @@ def tile_list_reed_bench_page_kernel(
         def product_a(s):
             g, t = divmod(s, PACK)
             for h in range(HALVES):
-                cols = slice(h * BANK, (h + 1) * BANK)
-                a_ps[s, h] = psum.tile([P, BANK], F32, name="a_ps", tag="a_ps")
+                a_ps[s, h] = bank(s, h, 1)
                 for a in range(PASSES):
                     nc.tensor.matmul_mx(
                         out=a_ps[s, h][:], lhsT=w1_c[g, a][:, t * P : (t + 1) * P].bitcast(FP8X4),
                         lhsT_scale=w1_s[g, a][:, t * P : (t + 1) * P],
-                        rhs=v_w[h][:, a, :].bitcast(FP8X4), rhs_scale=v_s[h][:, a, :],
+                        rhs=v_w[h][:, a, :].bitcast(FP8X4), rhs_scale=v_s[0][4 * a : P, h * BANK : (h + 1) * BANK],
                         start=(a == 0), stop=(a == PASSES - 1),
                     )
             if s >= 2:
@@ -237,7 +246,7 @@ def tile_list_reed_bench_page_kernel(
 
         def weigh(s):
             t = s % PACK
-            w_rows = wgs_first[:] if t == 0 else wgs_rest[:, t - 1, :]
+            w_rows = wgs_sb[t]
             if s + 1 < SLICES:
                 val[s] = b_tile[s + 1]
             else:
@@ -291,24 +300,30 @@ def tile_list_reed_bench_page_kernel(
 
         def weave_page(g, c):
             y_woven[g, c] = ring.tile([P, PACK * BANK], BF16, name="woven", tag="woven", bufs=4, align_bytes=64)
-            on_vector = g == GROUPS - 1 and c > 0
-            cols = slice(c * BANK, (c + 1) * BANK)
-            weave(nc.vector.tensor_copy if on_vector else nc.scalar.copy, y_woven[g, c][:], page_bf[g][:, :, cols])
+            on_scalar = BANK if g == 0 else min(max(TAIL_ON_SCALAR - c * BANK, 0), BANK)
+            for engine_copy, lo, hi in ((nc.scalar.copy, 0, on_scalar), (nc.vector.tensor_copy, on_scalar, BANK)):
+                if hi > lo:
+                    weave(
+                        engine_copy,
+                        y_woven[g, c][:, PACK * lo : PACK * hi],
+                        page_bf[g][:, :, c * BANK + lo : c * BANK + hi],
+                    )
 
         def planes(g, chunks, tag):
             if chunks[0] == 0:
-                y_s[g] = ring.tile([P, T2], U8, name="y_s", bufs=1, align_bytes=64)
+                y_s[g] = ring.tile([P, BANK], U8, name="y_s", bufs=1, align_bytes=64)
             words_out = out_2[g].rearrange("p m t -> p (m t)").bitcast(I32)
             y_c = keep.tile([P, len(chunks) * BANK], U32, name="y_c", tag=tag, align_bytes=64)
             for i, c in enumerate(chunks):
                 cols = slice(c * BANK, (c + 1) * BANK)
                 words = y_c[:, i * BANK : (i + 1) * BANK]
-                nc.vector.quantize_mx(out=words.bitcast(FP8X4), scales=y_s[g][:, cols], in_=y_woven[g, c][:])
+                nc.vector.quantize_mx(out=words.bitcast(FP8X4), scales=y_s[g][4 * c : P, :], in_=y_woven[g, c][:])
                 nc.sync.dma_start(words_out[:, cols], words.bitcast(I32))
             if chunks[-1] == CHUNKS - 1:
                 for q in range(4):
                     nc.sync.dma_start(
-                        out_3[g, 4 * q : 4 * q + 4, :].bitcast(I32), y_s[g][32 * q : 32 * q + 4, :].bitcast(I32)
+                        out_3[g, 4 * q : 4 * q + 4, :].rearrange("r (c w) -> c r w", c=CHUNKS).bitcast(I32),
+                        y_s[g][32 * q : 32 * q + 4 * CHUNKS, :].bitcast(I32),
                     )
 
         w3_s = keep.tile([P, GROUPS * N], U8, name="w3_s", align_bytes=64)
@@ -333,17 +348,20 @@ def tile_list_reed_bench_page_kernel(
                 )
             nc.vector.tensor_scalar(turns[:], span_sb[:], 1.0 / (2.0 * math.pi), None, ALU.mult)
 
-        product_b(0)
-        product_b(1)
+        for h in range(HALVES):
+            product_b(0, h)
+            product_b(1, h)
         product_a(0)
         deal_w2(1)
-        product_b(2)
         combine(0)
         for s in range(SLICES):
             if s + 2 < SLICES:
                 load_page(s + 2)
-            if s + 3 < SLICES:
-                product_b(s + 3)
+            if s == 0:
+                load_wgs(3)
+            if s + 2 < SLICES:
+                for h in range(HALVES):
+                    product_b(s + 2, h)
             if s + 1 < SLICES:
                 make_gate(s + 1)
                 product_a(s + 1)
@@ -375,7 +393,7 @@ def tile_list_reed_bench_page_kernel(
 
         weave_x(1)
         quantize_x(1)
-        g_ps = [psum.tile([P, BANK], F32, name="g_ps", tag="b_ps") for c in range(NT)]
+        g_ps = [bank(SLICES - 2 + c // HALVES, c % HALVES, 0) for c in range(NT)]
         for g in range(GROUPS):
             for c in range(NT):
                 cols = slice(g * N + c * P, g * N + (c + 1) * P)

@@ -49,12 +49,10 @@ def tile_list_reed_bench_page_kernel(
         idx = lists.tile([P, S // 16], U16, name="idx")
         idx2 = lists.tile([P, S // 16], U16, name="idx2")
         idx3 = lists.tile([P, PK // 16], U16, name="idx3")
-        tab_s = keep.tile([P, T], U8, name="tab_s", align_bytes=64)
-        v_s = [keep.tile([P, S], U8, name="v_s%d" % a, align_bytes=64) for a in range(PASSES)]
-        w2_s = late.tile([P, PASSES, H], U8, name="w2_s", align_bytes=64, offset=0)
-        nc.gpsimd.memset(tab_s[:].bitcast(I32), 0)
+        tab_s = keep.tile([P, PASSES, T], U8, name="tab_s", align_bytes=64)
+        w2_s = late.tile([P, PASSES, H], U8, name="w2_s", align_bytes=64, offset=3072)
+        nc.gpsimd.memset(tab_s[:].rearrange("p a c -> p (a c)").bitcast(I32), 0)
         nc.gpsimd.memset(w2_s[:].rearrange("p a c -> p (a c)").bitcast(I32), 0)
-        nc.gpsimd.memset(v_s[1][:].bitcast(I32), 0)
         warm = keep.tile([P, 1], F32, name="warm")
         nc.vector.memset(warm[:], 0.0)
         nc.scalar.activation(warm[:], warm[:], ACT.Silu)
@@ -106,8 +104,8 @@ def tile_list_reed_bench_page_kernel(
         load_tab(0)
         for q in range(4):
             nc.sync.dma_start(
-                tab_s[32 * q : 32 * q + 4 * PASSES, :].bitcast(I32),
-                tab_scales[:, 4 * q : 4 * q + 4, :].bitcast(I32),
+                tab_s[32 * q : 32 * q + 4].bitcast(I32),
+                tab_scales[:, 4 * q : 4 * q + 4, :].rearrange("a r c -> r a c").bitcast(I32),
             )
         load_tab(1)
         for q in range(4):
@@ -128,19 +126,16 @@ def tile_list_reed_bench_page_kernel(
         load_page(1)
         load_wgs(2)
 
-        v_w = {}
-        nc.vector.tensor_copy(v_s[0][:], tab_s[:].indirect(idx[:]))
-        for q in range(4):
-            nc.scalar.dma_start(
-                v_s[1][32 * q : 32 * q + 4, :].bitcast(I32), v_s[0][32 * q + 4 : 32 * q + 8, :].bitcast(I32)
-            )
+        v_w, v_s = {}, {}
 
         def gather_table(h):
             entries = idx[:, h * BANK // 16 : (h + 1) * BANK // 16]
             for a in range(PASSES):
+                nc.vector.tensor_copy(v_s[h][:, a, :], tab_s[:, a, :].indirect(entries))
                 nc.vector.tensor_copy(v_w[h][:, a, :], tab_w[a][:].bitcast(U32).indirect(entries))
 
         v_w[0] = keep.tile([P, PASSES, BANK], U32, name="v_w0", align_bytes=64)
+        v_s[0] = keep.tile([P, PASSES, BANK], U8, name="v_s0", align_bytes=64)
         gather_table(0)
         w2_sd = keep.tile([P, PASSES, SLICES, P], U8, name="w2_sd", align_bytes=64)
         nc.vector.tensor_copy(
@@ -156,6 +151,7 @@ def tile_list_reed_bench_page_kernel(
 
         deal_w2(0)
         v_w[1] = late.tile([P, PASSES, BANK], U32, name="v_w1", align_bytes=64, offset=0)
+        v_s[1] = late.tile([P, PASSES, BANK], U8, name="v_s1", align_bytes=64, offset=4096)
         gather_table(1)
 
         w1_c, w1_s = {}, {}
@@ -189,33 +185,29 @@ def tile_list_reed_bench_page_kernel(
             return [slice(h * BANK, (h + 1) * BANK) for h in range(HALVES)] if s == 0 else [slice(0, S)]
 
         def bank(s, h, which):
-            pair = 2 * ((s // 2 + which) % 2) + s % 2
+            pair = 2 * which + s % 2
             return psum.tile([P, BANK], F32, name="acc", tag="bank%d" % (2 * pair + h))
 
         def product_b(s, h):
             g, t = divmod(s, PACK)
-            if h == 0:
-                if s == 0:
-                    gate[s] = ring.tile([P, S], F32, name="gate")
-                else:
-                    b_tile[s] = ring.tile([P, S], F32, name="b_sb", tag="b_sb", bufs=3)
+            if h == 0 and s >= 2:
+                b_tile[s] = ring.tile([P, S], F32, name="b_sb", tag="b_sb", bufs=3)
             cols = slice(h * BANK, (h + 1) * BANK)
             b_ps = bank(s, h, 0)
             for a in range(PASSES):
                 nc.tensor.matmul_mx(
                     out=b_ps[:], lhsT=w2_wd[g][:, a, t, :].bitcast(FP4X4), lhsT_scale=w2_sd[:, a, s, :],
-                    rhs=v_w[h][:, a, :].bitcast(FP8X4), rhs_scale=v_s[a][:, cols],
+                    rhs=v_w[h][:, a, :].bitcast(FP8X4), rhs_scale=v_s[h][:, a, :],
                     start=(a == 0), stop=(a == PASSES - 1),
                 )
-            if s == 0:
+            if s < 2:
                 nc.vector.tensor_tensor(gate[s][:, cols], b_ps[:], alloy_sb[s][:, cols], ALU.mult)
             else:
                 nc.scalar.copy(b_tile[s][:, cols], b_ps[:])
 
         def make_gate(s):
             gate[s] = ring.tile([P, S], F32, name="gate")
-            for cols in parts(s - 1):
-                nc.gpsimd.tensor_tensor(gate[s][:, cols], b_tile[s][:, cols], alloy_sb[s][:, cols], ALU.mult)
+            nc.gpsimd.tensor_tensor(gate[s][:], b_tile[s][:], alloy_sb[s][:], ALU.mult)
 
         def product_a(s):
             g, t = divmod(s, PACK)
@@ -225,7 +217,7 @@ def tile_list_reed_bench_page_kernel(
                     nc.tensor.matmul_mx(
                         out=a_ps[s, h][:], lhsT=w1_c[g, a][:, t * P : (t + 1) * P].bitcast(FP8X4),
                         lhsT_scale=w1_s[g, a][:, t * P : (t + 1) * P],
-                        rhs=v_w[h][:, a, :].bitcast(FP8X4), rhs_scale=v_s[0][4 * a : P, h * BANK : (h + 1) * BANK],
+                        rhs=v_w[h][:, a, :].bitcast(FP8X4), rhs_scale=v_s[h][:, a, :],
                         start=(a == 0), stop=(a == PASSES - 1),
                     )
             if s >= 2:
@@ -247,7 +239,7 @@ def tile_list_reed_bench_page_kernel(
         def weigh(s):
             t = s % PACK
             w_rows = wgs_sb[t]
-            if s + 1 < SLICES:
+            if 0 < s < SLICES - 1:
                 val[s] = b_tile[s + 1]
             else:
                 val[s] = ring.tile([P, S], F32, name="val", tag="b_sb", bufs=3)
@@ -268,7 +260,7 @@ def tile_list_reed_bench_page_kernel(
                 page_bf[g] = ring.tile([P, PACK, T2], BF16, name="page_bf", bufs=1)
                 x_bf[g] = ring.tile([P, PACK, PK], BF16, name="x_bf", bufs=1)
             nc.vector.tensor_scalar(x_bf[g][:, t, :], picked[:], tau_sb[:, g, t : t + 1], None, ALU.max)
-            nc.sync.dma_start(dealt(out_1, s), page[s][:])
+            nc.scalar.dma_start(dealt(out_1, s), page[s][:])
             if s == SLICES - 1:
                 for c in range(CHUNKS):
                     cols = slice(c * BANK, (c + 1) * BANK)
@@ -348,24 +340,31 @@ def tile_list_reed_bench_page_kernel(
                 )
             nc.vector.tensor_scalar(turns[:], span_sb[:], 1.0 / (2.0 * math.pi), None, ALU.mult)
 
+        first_gates = keep.tile([P, 2, S], F32, name="first_gates", tag="after0", align_bytes=64)
+        gate[0], gate[1] = first_gates[:, 0, :], first_gates[:, 1, :]
         for h in range(HALVES):
             product_b(0, h)
             product_b(1, h)
         product_a(0)
         deal_w2(1)
         combine(0)
+        weigh(0)
+        for h in range(HALVES):
+            product_b(2, h)
         for s in range(SLICES):
             if s + 2 < SLICES:
                 load_page(s + 2)
             if s == 0:
                 load_wgs(3)
-            if s + 2 < SLICES:
+            if s + 3 < SLICES:
                 for h in range(HALVES):
-                    product_b(s + 2, h)
-            if s + 1 < SLICES:
+                    product_b(s + 3, h)
+            if 0 < s < SLICES - 1:
                 make_gate(s + 1)
+            if s + 1 < SLICES:
                 product_a(s + 1)
-            weigh(s)
+            if s > 0:
+                weigh(s)
             if s + 1 < SLICES:
                 combine(s + 1)
             if s + 3 < SLICES:

import math
from contextlib import ExitStack

import concourse.mybir as mybir

K, H, N, T, S, T2, PK = 1024, 1024, 384, 2048, 1024, 2048, 512
FLOPS = 2 * K * H * S * 2 + 2 * H * N * PK

F32 = mybir.dt.float32
BF16 = mybir.dt.bfloat16
I32 = mybir.dt.int32
U32 = mybir.dt.uint32
U16 = mybir.dt.uint16
U8 = mybir.dt.uint8
FP8X4 = mybir.dt.float8_e4m3fn_x4
FP4X4 = mybir.dt.float4_e2m1fn_x4
ALU = mybir.AluOpType
ACT = mybir.ActivationFunctionType

P = 128
PACK = 4
GROUP = P * PACK
BANK = 512
PASSES = K // GROUP
GROUPS = H // GROUP
SLICES = GROUPS * PACK
HALVES = S // BANK
CHUNKS = T2 // BANK
NT = N // P
TAIL_ON_SCALAR = 768


def tile_list_reed_bench_page_kernel(
    tc, tab_words, tab_scales, offs, w1, w2_words, w2_scales, alloy, page0, wgs, offs2, offs3, tau, w3, span,
    out_0, out_1, out_2, out_3,
):
    nc = tc.nc
    with ExitStack() as ctx:
        lists = ctx.enter_context(tc.tile_pool(name="lists", bufs=1))
        keep = ctx.enter_context(tc.tile_pool(name="keep", bufs=1))
        ring = ctx.enter_context(tc.tile_pool(name="ring", bufs=2))
        late = ctx.enter_context(tc.tile_pool(name="late", bufs=1))
        psum = ctx.enter_context(tc.psum_pool(name="psum", bufs=1))

        def dealt(mat, s):
            g, t = divmod(s, PACK)
            return mat[g * GROUP : (g + 1) * GROUP, :].rearrange("(p t) c -> t p c", t=PACK)[t]

        idx = lists.tile([P, S // 16], U16, name="idx")
        idx2 = lists.tile([P, S // 16], U16, name="idx2")
        idx3 = lists.tile([P, PK // 16], U16, name="idx3")
        tab_s = keep.tile([P, PASSES, T], U8, name="tab_s", align_bytes=64)
        w2_s = late.tile([P, PASSES, H], U8, name="w2_s", align_bytes=64, offset=3072)
        nc.gpsimd.memset(tab_s[:].rearrange("p a c -> p (a c)").bitcast(I32), 0)
        nc.gpsimd.memset(w2_s[:].rearrange("p a c -> p (a c)").bitcast(I32), 0)
        warm = keep.tile([P, 1], F32, name="warm")
        nc.vector.memset(warm[:], 0.0)
        nc.scalar.activation(warm[:], warm[:], ACT.Silu)

        w2_w = [keep.tile([P, PASSES, 2 * GROUP], U8, name="w2_w%d" % g, align_bytes=64) for g in range(GROUPS)]

        def load_w2(g):
            cols = w2_words[:, :, 2 * g * GROUP : 2 * (g + 1) * GROUP]
            nc.sync.dma_start(w2_w[g][:].bitcast(I32), cols.rearrange("a p c -> p a c").bitcast(I32))

        tab_w = [keep.tile([P, T], I32, name="tab_w%d" % a, align_bytes=64) for a in range(PASSES)]

        def load_tab(a):
            nc.sync.dma_start(tab_w[a][:], tab_words[a].rearrange("p c i -> p (c i)").bitcast(I32))

        w_raw = {}

        def load_w1(g, a):
            w_raw[g, a] = ring.tile([P, PACK, GROUP], F32, name="w_raw", tag="w_raw", bufs=3)
            rows = w1[a * GROUP : (a + 1) * GROUP, g * GROUP : (g + 1) * GROUP]
            nc.sync.dma_start(w_raw[g, a][:], rows.rearrange("(p j) c -> p j c", j=PACK))

        alloy_sb, page = {}, {}

        def load_alloy(s):
            alloy_sb[s] = ring.tile([P, S], F32, name="alloy_sb", tag="alloy_sb", bufs=3)
            nc.sync.dma_start(alloy_sb[s][:], dealt(alloy, s))

        def load_page(s):
            page[s] = ring.tile([P, T2], F32, name="page", bufs=4)
            nc.sync.dma_start(page[s][:], dealt(page0, s))

        wgs_sb = [keep.tile([P, S], F32, name="wgs_sb%d" % t) for t in range(PACK)]

        def load_wgs(t):
            for q in (0, 2, 1, 3):
                nc.sync.dma_start(wgs_sb[t][32 * q : 32 * q + 32, :], wgs.rearrange("(p t) c -> t p c", t=PACK)[t])

        nc.sync.dma_start(idx[:], offs)
        nc.sync.dma_start(idx2[:], offs2)
        nc.sync.dma_start(idx3[:], offs3)
        tau_sb = keep.tile([P, GROUPS, PACK], F32, name="tau_sb")
        nc.sync.dma_start(tau_sb[:], tau.rearrange("(g p t) -> p g t", g=GROUPS, t=PACK))
        span_sb = keep.tile([P, NT], F32, name="span_sb")
        with nc.allow_non_contiguous_dma(reason="one value of span for each partition"):
            nc.sync.dma_start(span_sb[:], span.rearrange("(c p) -> p c", p=P))
        load_w2(0)
        load_w2(1)
        load_tab(0)
        for q in range(4):
            nc.sync.dma_start(
                tab_s[32 * q : 32 * q + 4].bitcast(I32),
                tab_scales[:, 4 * q : 4 * q + 4, :].rearrange("a r c -> r a c").bitcast(I32),
            )
        load_tab(1)
        for q in range(4):
            nc.sync.dma_start(
                w2_s[32 * q : 32 * q + 4].bitcast(I32),
                w2_scales[:, 4 * q : 4 * q + 4, :].rearrange("a r c -> r a c").bitcast(I32),
            )
        load_w1(0, 0)
        load_w1(0, 1)
        load_alloy(0)
        load_alloy(1)
        load_wgs(0)
        load_page(0)
        load_alloy(2)
        load_wgs(1)
        load_w1(1, 0)
        load_w1(1, 1)
        load_page(1)
        load_wgs(2)

        v_w, v_s = {}, {}

        def gather_table(h):
            entries = idx[:, h * BANK // 16 : (h + 1) * BANK // 16]
            for a in range(PASSES):
                nc.vector.tensor_copy(v_s[h][:, a, :], tab_s[:, a, :].indirect(entries))
                nc.vector.tensor_copy(v_w[h][:, a, :], tab_w[a][:].bitcast(U32).indirect(entries))

        v_w[0] = keep.tile([P, PASSES, BANK], U32, name="v_w0", align_bytes=64)
        v_s[0] = keep.tile([P, PASSES, BANK], U8, name="v_s0", align_bytes=64)
        gather_table(0)
        w2_sd = keep.tile([P, PASSES, SLICES, P], U8, name="w2_sd", align_bytes=64)
        nc.vector.tensor_copy(
            w2_sd[:].rearrange("p a (g t) m -> p (a g) t m", t=PACK),
            w2_s[:].rearrange("p a (g m t) -> p (a g) t m", g=GROUPS, t=PACK),
        )
        w2_wd = [keep.tile([P, PASSES, PACK, 2 * P], U8, name="w2_wd%d" % g, align_bytes=64) for g in range(GROUPS)]

        def deal_w2(g):
            nc.vector.tensor_copy(
                w2_wd[g][:].bitcast(U16), w2_w[g][:].bitcast(U16).rearrange("p a (m t) -> p a t m", t=PACK)
            )

        deal_w2(0)
        v_w[1] = late.tile([P, PASSES, BANK], U32, name="v_w1", align_bytes=64, offset=0)
        v_s[1] = late.tile([P, PASSES, BANK], U8, name="v_s1", align_bytes=64, offset=4096)
        gather_table(1)

        w1_c, w1_s = {}, {}

        w1_bf = {}
        width = PACK * GROUP

        def weave_w1(g):
            w1_bf[g] = keep.tile([P, PASSES * width], BF16, name="w1_bf", tag="after0", align_bytes=64)
            for a in range(PASSES):
                nc.scalar.copy(
                    w1_bf[g][:, a * width : (a + 1) * width].rearrange("p (t m j) -> p m j t", t=PACK, j=PACK),
                    w_raw[g, a][:].rearrange("p j (m t) -> p m j t", t=PACK),
                )

        def quantize_w1(g):
            codes = keep.tile([P, PASSES * GROUP], U32, name="w1_c", tag="after1" if g else "w1_c", align_bytes=64)
            for a in range(PASSES):
                w1_c[g, a] = codes[:, a * GROUP : (a + 1) * GROUP]
                w1_s[g, a] = keep.tile([P, GROUP], U8, name="w1_s%d%d" % (g, a), align_bytes=64)
                nc.vector.quantize_mx(
                    out=w1_c[g, a].bitcast(FP8X4), scales=w1_s[g, a][:], in_=w1_bf[g][:, a * width : (a + 1) * width]
                )

        weave_w1(0)
        quantize_w1(0)

        a_ps, gate, hval, val, b_tile, a_sb = {}, {}, {}, {}, {}, {}

        def parts(s):
            return [slice(h * BANK, (h + 1) * BANK) for h in range(HALVES)] if s == 0 else [slice(0, S)]

        def bank(s, h, which):
            pair = 2 * which + s % 2
            return psum.tile([P, BANK], F32, name="acc", tag="bank%d" % (2 * pair + h))

        def product_b(s, h):
            g, t = divmod(s, PACK)
            if h == 0 and s >= 2:
                b_tile[s] = ring.tile([P, S], F32, name="b_sb", tag="b_sb", bufs=3)
            cols = slice(h * BANK, (h + 1) * BANK)
            b_ps = bank(s, h, 0)
            for a in range(PASSES):
                nc.tensor.matmul_mx(
                    out=b_ps[:], lhsT=w2_wd[g][:, a, t, :].bitcast(FP4X4), lhsT_scale=w2_sd[:, a, s, :],
                    rhs=v_w[h][:, a, :].bitcast(FP8X4), rhs_scale=v_s[h][:, a, :],
                    start=(a == 0), stop=(a == PASSES - 1),
                )
            if s < 2:
                nc.vector.tensor_tensor(gate[s][:, cols], b_ps[:], alloy_sb[s][:, cols], ALU.mult)
            else:
                nc.scalar.copy(b_tile[s][:, cols], b_ps[:])

        def make_gate(s):
            gate[s] = ring.tile([P, S], F32, name="gate")
            nc.gpsimd.tensor_tensor(gate[s][:], b_tile[s][:], alloy_sb[s][:], ALU.mult)

        def product_a(s):
            g, t = divmod(s, PACK)
            for h in range(HALVES):
                a_ps[s, h] = bank(s, h, 1)
                for a in range(PASSES):
                    nc.tensor.matmul_mx(
                        out=a_ps[s, h][:], lhsT=w1_c[g, a][:, t * P : (t + 1) * P].bitcast(FP8X4),
                        lhsT_scale=w1_s[g, a][:, t * P : (t + 1) * P],
                        rhs=v_w[h][:, a, :].bitcast(FP8X4), rhs_scale=v_s[h][:, a, :],
                        start=(a == 0), stop=(a == PASSES - 1),
                    )
            if s >= 2:
                a_sb[s] = ring.tile([P, BANK], F32, name="a_sb", bufs=1)
                nc.scalar.copy(a_sb[s][:], a_ps[s, 1][:])

        def combine(s):
            hval[s] = ring.tile([P, S], F32, name="hval", tag="hval")
            for h in range(HALVES):
                cols = slice(h * BANK, (h + 1) * BANK)
                if h == 0 or s < 2:
                    nc.vector.scalar_tensor_tensor(
                        hval[s][:, cols], gate[s][:, cols], 1.0, a_ps[s, h][:], ALU.add, ALU.mult
                    )
                else:
                    nc.scalar.activation(gate[s][:, cols], gate[s][:, cols], ACT.Identity, bias=1.0)
                    nc.gpsimd.tensor_tensor(hval[s][:, cols], gate[s][:, cols], a_sb[s][:], ALU.mult)

        def weigh(s):
            t = s % PACK
            w_rows = wgs_sb[t]
            if 0 < s < SLICES - 1:
                val[s] = b_tile[s + 1]
            else:
                val[s] = ring.tile([P, S], F32, name="val", tag="b_sb", bufs=3)
            for cols in parts(s):
                nc.gpsimd.tensor_tensor(val[s][:, cols], hval[s][:, cols], w_rows[:, cols], ALU.mult)

        page_bf, x_bf = {}, {}

        def place(s):
            g, t = divmod(s, PACK)
            for cols in parts(s):
                nc.vector.tensor_copy(
                    page[s][:].indirect(idx2[:, cols.start // 16 : cols.stop // 16]), val[s][:, cols]
                )
            picked = keep.tile([P, PK], F32, name="picked", tag="after%d" % (s if s < SLICES - 1 else 2), align_bytes=64)
            nc.vector.tensor_copy(picked[:], page[s][:].indirect(idx3[:]))
            if t == 0:
                page_bf[g] = ring.tile([P, PACK, T2], BF16, name="page_bf", bufs=1)
                x_bf[g] = ring.tile([P, PACK, PK], BF16, name="x_bf", bufs=1)
            nc.vector.tensor_scalar(x_bf[g][:, t, :], picked[:], tau_sb[:, g, t : t + 1], None, ALU.max)
            nc.scalar.dma_start(dealt(out_1, s), page[s][:])
            if s == SLICES - 1:
                for c in range(CHUNKS):
                    cols = slice(c * BANK, (c + 1) * BANK)
                    nc.scalar.copy(page_bf[g][:, t, cols], page[s][:, cols])
            else:
                nc.scalar.copy(page_bf[g][:, t, :], page[s][:])

        def weave(engine_copy, dst, src):
            engine_copy(
                dst.rearrange("p (c i t) -> p c t i", i=PACK, t=PACK),
                src.rearrange("p t (c i) -> p c t i", i=PACK),
            )

        x_c, x_s = {}, {}

        x_woven = {}

        def weave_x(g):
            x_woven[g] = keep.tile([P, PACK * PK], BF16, name="x_woven", align_bytes=64)
            weave(nc.vector.tensor_copy if g == GROUPS - 1 else nc.scalar.copy, x_woven[g][:], x_bf[g][:])

        def quantize_x(g):
            woven = x_woven[g]
            x_c[g] = keep.tile([P, PK], U32, name="x_c", tag="x_c" if g else "after4", align_bytes=64)
            x_s[g] = keep.tile([P, PK], U8, name="x_s%d" % g, align_bytes=64)
            nc.vector.quantize_mx(out=x_c[g][:].bitcast(FP8X4), scales=x_s[g][:], in_=woven[:])

        y_s, y_woven = {}, {}

        def weave_page(g, c):
            y_woven[g, c] = ring.tile([P, PACK * BANK], BF16, name="woven", tag="woven", bufs=4, align_bytes=64)
            on_scalar = BANK if g == 0 else min(max(TAIL_ON_SCALAR - c * BANK, 0), BANK)
            for engine_copy, lo, hi in ((nc.scalar.copy, 0, on_scalar), (nc.vector.tensor_copy, on_scalar, BANK)):
                if hi > lo:
                    weave(
                        engine_copy,
                        y_woven[g, c][:, PACK * lo : PACK * hi],
                        page_bf[g][:, :, c * BANK + lo : c * BANK + hi],
                    )

        def planes(g, chunks, tag):
            if chunks[0] == 0:
                y_s[g] = ring.tile([P, BANK], U8, name="y_s", bufs=1, align_bytes=64)
            words_out = out_2[g].rearrange("p m t -> p (m t)").bitcast(I32)
            y_c = keep.tile([P, len(chunks) * BANK], U32, name="y_c", tag=tag, align_bytes=64)
            for i, c in enumerate(chunks):
                cols = slice(c * BANK, (c + 1) * BANK)
                words = y_c[:, i * BANK : (i + 1) * BANK]
                nc.vector.quantize_mx(out=words.bitcast(FP8X4), scales=y_s[g][4 * c : P, :], in_=y_woven[g, c][:])
                nc.sync.dma_start(words_out[:, cols], words.bitcast(I32))
            if chunks[-1] == CHUNKS - 1:
                for q in range(4):
                    nc.sync.dma_start(
                        out_3[g, 4 * q : 4 * q + 4, :].rearrange("r (c w) -> c r w", c=CHUNKS).bitcast(I32),
                        y_s[g][32 * q : 32 * q + 4 * CHUNKS, :].bitcast(I32),
                    )

        w3_s = keep.tile([P, GROUPS * N], U8, name="w3_s", align_bytes=64)
        w3_t = {}
        turns = keep.tile([P, NT], F32, name="turns")

        def weave_w3():
            w3_bf = keep.tile([P, GROUPS * N * PACK], BF16, name="w3_bf", tag="after2", align_bytes=64)
            w3_t["bf"] = w3_bf
            for g in range(GROUPS):
                raw = ring.tile([P, PACK, N], F32, name="w_raw", tag="w_raw", bufs=3)
                nc.sync.dma_start(raw[:], w3[g * GROUP : (g + 1) * GROUP, :].rearrange("(p j) c -> p j c", j=PACK))
                weave(nc.scalar.copy, w3_bf[:, g * N * PACK : (g + 1) * N * PACK], raw[:])

        def quantize_w3():
            w3_bf = w3_t["bf"]
            w3_c = keep.tile([P, GROUPS * N], U32, name="w3_c", tag="after3", align_bytes=64)
            w3_t["c"] = w3_c
            for lo, hi in ((0, BANK), (BANK, GROUPS * N)):
                nc.vector.quantize_mx(
                    out=w3_c[:, lo:hi].bitcast(FP8X4), scales=w3_s[:, lo:hi], in_=w3_bf[:, PACK * lo : PACK * hi]
                )
            nc.vector.tensor_scalar(turns[:], span_sb[:], 1.0 / (2.0 * math.pi), None, ALU.mult)

        first_gates = keep.tile([P, 2, S], F32, name="first_gates", tag="after0", align_bytes=64)
        gate[0], gate[1] = first_gates[:, 0, :], first_gates[:, 1, :]
        for h in range(HALVES):
            product_b(0, h)
            product_b(1, h)
        product_a(0)
        deal_w2(1)
        combine(0)
        weigh(0)
        for h in range(HALVES):
            product_b(2, h)
        for s in range(SLICES):
            if s + 2 < SLICES:
                load_page(s + 2)
            if s == 0:
                load_wgs(3)
            if s + 3 < SLICES:
                for h in range(HALVES):
                    product_b(s + 3, h)
            if 0 < s < SLICES - 1:
                make_gate(s + 1)
            if s + 1 < SLICES:
                product_a(s + 1)
            if s > 0:
                weigh(s)
            if s + 1 < SLICES:
                combine(s + 1)
            if s + 3 < SLICES:
                load_alloy(s + 3)
            place(s)
            if s == 0:
                weave_w1(1)
            if s == 1:
                quantize_w1(1)
            if s == 2:
                weave_w3()
            if s == PACK - 1:
                quantize_w3()
            if s == PACK:
                weave_x(0)
                quantize_x(0)
            if s == PACK + 1:
                weave_page(0, 0)
                weave_page(0, 1)
                planes(0, [0, 1], "after5")
            if s == PACK + 2:
                weave_page(0, 2)
                weave_page(0, 3)
                planes(0, [2, 3], "after6")

        weave_x(1)
        quantize_x(1)
        g_ps = [bank(SLICES - 2 + c // HALVES, c % HALVES, 0) for c in range(NT)]
        for g in range(GROUPS):
            for c in range(NT):
                cols = slice(g * N + c * P, g * N + (c + 1) * P)
                nc.tensor.matmul_mx(
                    out=g_ps[c][:], lhsT=w3_t["c"][:, cols].bitcast(FP8X4), lhsT_scale=w3_s[:, cols],
                    rhs=x_c[g][:].bitcast(FP8X4), rhs_scale=x_s[g][:],
                    start=(g == 0), stop=(g == GROUPS - 1),
                )
        for c in range(NT):
            th = ring.tile([P, PK], F32, name="th", tag="alloy_sb", bufs=3)
            nc.scalar.activation(th[:], g_ps[c][:], ACT.Tanh)
            whole = ring.tile([P, PK], I32, name="whole", tag="b_sb", bufs=3)
            nc.vector.tensor_scalar(whole[:], th[:], turns[:, c : c + 1], None, ALU.mult)
            rest = ring.tile([P, PK], F32, name="rest", tag="hval")
            nc.vector.scalar_tensor_tensor(rest[:], th[:], turns[:, c : c + 1], whole[:], ALU.mult, ALU.subtract)
            nc.scalar.activation(th[:], rest[:], ACT.Abs)
            y = ring.tile([P, PK], F32, name="y", tag="w_raw", bufs=3)
            nc.scalar.activation(y[:], th[:], ACT.Sin, bias=math.pi / 2.0, scale=-2.0 * math.pi)
            nc.sync.dma_start(out_0[c * P : (c + 1) * P, :], y[:])
        for c in range(CHUNKS):
            weave_page(1, c)
        planes(1, [0, 1], "after5")
        planes(1, [2, 3], "after0")
